import numpy as np
import ml_dtypes


def mxq(x, axis, fmt="e4m3"):
    dtype, down = {"e4m3": (ml_dtypes.float8_e4m3fn, 7), "e5m2": (ml_dtypes.float8_e5m2, 14)}[fmt]
    v = np.moveaxis(np.asarray(x, np.float32).astype(ml_dtypes.bfloat16).astype(np.float64), axis, -1)
    blocks = v.reshape(v.shape[:-1] + (-1, 32))
    amax = np.abs(blocks).max(-1, keepdims=True)
    byte = np.maximum(np.where(amax > 0, np.frexp(amax)[1] - 1 + 127, 0) - down, 1)
    scale = np.exp2(byte - 127.0)
    codes = (blocks / scale).astype(np.float32).astype(dtype).astype(np.float64)
    return np.moveaxis((codes * scale).reshape(v.shape), -1, axis)


WIDE = False


def mx_kscale(k):
    if not WIDE:
        return np.ones(k)
    levels = np.array([10, -10, 5, -5, 0])
    if k % 512:
        return np.exp2(np.random.permutation(np.resize(levels, k // 32))).repeat(32)
    a = np.empty((k // 512, 16))
    for p in range(k // 512):
        a[p, :8] = np.random.permutation(np.resize(levels, 8))
        for g in range(8):
            far = levels[np.abs(levels - a[p, g]) >= 10]
            a[p, g + 8] = far[np.random.randint(len(far))]
    return np.exp2(a.ravel()).repeat(32)


def f64(x):
    return np.asarray(x).astype(np.float64)


def striped8(idx):
    return np.asarray(idx).reshape(8, -1, 16).transpose(0, 2, 1).reshape(128, -1).astype(np.uint16)


def unstriped8(offs):
    return offs.reshape(8, 16, -1).transpose(0, 2, 1).reshape(8, -1).astype(np.int64)


def pick8(x, idx, run):
    r = np.arange(len(x))
    return x[r[:, None], idx[r % (8 * run) // run]]


E2M1 = np.array([0.0, 0.5, 1.0, 1.5, 2.0, 3.0, 4.0, 6.0, -0.0, -0.5, -1.0, -1.5, -2.0, -3.0, -4.0, -6.0])


def pack_weight(w, fmt):
    k, n = w.shape
    w = f64(np.asarray(w, np.float32).astype(ml_dtypes.bfloat16)).reshape(k // 32, 32, n)
    amax = np.abs(w).max(1)
    if fmt == "e4m3":
        byte = np.frexp(amax)[1] - 1 + 127 - 7
    else:
        mant, ex = np.frexp(amax / 6.0)
        byte = np.where(mant > 0.5, ex, ex - 1) + 127
    byte = np.clip(np.where(amax > 0, byte, 1), 1, 254)
    scaled = (w * np.exp2(127.0 - byte)[:, None, :]).reshape(k, n).astype(np.float32)
    by_word = np.ascontiguousarray(scaled.reshape(k // 512, 128, 4, n).transpose(0, 1, 3, 2))
    if fmt == "e4m3":
        words = by_word.astype(ml_dtypes.float8_e4m3fn).view(np.uint8)
    else:
        c = by_word.astype(ml_dtypes.float4_e2m1fn).view(np.uint8) & 0xF
        words = (c[..., 0::2] | (c[..., 1::2] << 4)).reshape(k // 512, 128, 2 * n)
    return np.ascontiguousarray(words), np.ascontiguousarray(byte.astype(np.uint8).reshape(k // 512, 16, n))


def unpack_weight(words, scales, fmt):
    g, _, n = scales.shape
    words = np.ascontiguousarray(words).reshape(g, 128, n, -1)
    if fmt == "e4m3":
        vals = words.view(ml_dtypes.float8_e4m3fn).astype(np.float64)
    else:
        nib = np.empty((g, 128, n, 4), np.uint8)
        nib[..., 0::2] = words & 0xF
        nib[..., 1::2] = words >> 4
        vals = E2M1[nib]
    vals = vals * np.repeat(np.exp2(scales.astype(np.float64) - 127.0), 8, axis=1)[..., None]
    return vals.transpose(0, 1, 3, 2).reshape(g * 512, n)


D, T, U, I, Q = 512, 1024, 1024, 512, 128


def setup_inputs():
    n = np.random.standard_normal
    idx = np.stack([np.random.permutation(T)[:I] for _ in range(8)])
    idx2 = np.stack([np.random.permutation(U)[:I] for _ in range(8)])
    idx3 = np.stack([np.random.permutation(T)[:I] for _ in range(8)])
    idx4 = np.stack([np.random.permutation(T)[:I] for _ in range(8)])
    fd = mx_kscale(D)
    keysp = pack_weight(n((D, T)) / fd[:, None], "e2m1")
    notesp = pack_weight(n((D, U)) / fd[:, None], "e4m3")
    return {
        "query": (n((D, Q)) * 1.0 / np.sqrt(D) * fd[:, None]).astype(np.float32),
        "keys_words": keysp[0],
        "keys_scales": keysp[1],
        "notes_words": notesp[0],
        "notes_scales": notesp[1],
        "offs": striped8(idx),
        "offs2": striped8(idx2),
        "offs3": striped8(idx3),
        "offs4": striped8(idx4),
    }


def reference(query, keys_words, keys_scales, notes_words, notes_scales, offs, offs2, offs3, offs4):
    idx = unstriped8(offs)
    idx2 = unstriped8(offs2)
    idx3 = unstriped8(offs3)
    idx4 = unstriped8(offs4)
    keysu = unpack_weight(keys_words, keys_scales, "e2m1")
    notesu = unpack_weight(notes_words, notes_scales, "e4m3")
    queryq = mxq(f64(query), 0, "e4m3")
    a = queryq.T @ keysu
    b = queryq.T @ notesu
    w = np.maximum(pick8(a, idx, 16), pick8(b, idx2, 16))
    v = np.maximum(pick8(a, idx3, 16), pick8(b, idx2, 16))
    m1 = np.minimum(w, v)
    f1 = np.zeros((Q, T))
    f1[np.arange(Q)[:, None], idx3[np.arange(Q) % 128 // 16]] = m1
    aa = a - f1
    y = pick8(aa, idx4, 16) + w
    return y

@@ -1,0 +1,135 @@
+from contextlib import ExitStack
+
+import concourse.mybir as mybir
+
+D, T, U, SLOTS, Q = 512, 1024, 1024, 512, 128
+FLOPS = 2 * Q * D * (T + U)
+
+F32 = mybir.dt.float32
+BF16 = mybir.dt.bfloat16
+I32 = mybir.dt.int32
+U32 = mybir.dt.uint32
+U16 = mybir.dt.uint16
+U8 = mybir.dt.uint8
+FP8X4 = mybir.dt.float8_e4m3fn_x4
+FP4X4 = mybir.dt.float4_e2m1fn_x4
+ALU = mybir.AluOpType
+COPY = mybir.ActivationFunctionType.Copy
+
+P = 128
+PACK = 4
+N = 256
+HALF = SLOTS // 2
+HCOLS = HALF // 16
+
+
+def tile_attend_betterworse_two_kernel(
+    tc, query, keys_words, keys_scales, notes_words, notes_scales, offs, offs2, offs3, offs4, out
+):
+    nc = tc.nc
+    with ExitStack() as ctx:
+        lists = ctx.enter_context(tc.tile_pool(name="lists", bufs=1))
+        sb = ctx.enter_context(tc.tile_pool(name="sb", bufs=1))
+        psum = ctx.enter_context(tc.psum_pool(name="psum", bufs=1))
+
+        key_plane = sb.tile([P, T], U8, name="key_plane", align_bytes=64)
+        note_plane = sb.tile([P, U], U8, name="note_plane", align_bytes=64)
+        f1 = sb.tile([P, T], F32, name="f1")
+        nc.vector.memset(key_plane[:].bitcast(U32), 0)
+        nc.vector.memset(note_plane[:].bitcast(U32), 0)
+        nc.vector.memset(f1[:], 0.0)
+
+        def load_scale_rows(plane, scales, r):
+            nc.sync.dma_start(out=plane[r:P:32, :].bitcast(I32), in_=scales[0, r:16:4, :].bitcast(I32))
+
+        q_raw = sb.tile([P, PACK, Q], F32, name="q_raw")
+        nc.sync.dma_start(out=q_raw[:], in_=query.rearrange("(p j) q -> p j q", j=PACK))
+        for r in range(4):
+            load_scale_rows(key_plane, keys_scales, r)
+        key_codes = sb.tile([P, 2 * T], U8, name="key_codes", align_bytes=64)
+        nc.sync.dma_start(out=key_codes[:].bitcast(I32), in_=keys_words[0].bitcast(I32))
+        note_codes = sb.tile([P, U], U32, name="note_codes", align_bytes=64)
+        nc.sync.dma_start(
+            out=note_codes[:].bitcast(I32), in_=notes_words[0].rearrange("p u j -> p (u j)").bitcast(I32)
+        )
+        for r in range(4):
+            load_scale_rows(note_plane, notes_scales, r)
+        idx1 = lists.tile([P, SLOTS // 16], U16, name="idx1")
+        idx3 = lists.tile([P, SLOTS // 16], U16, name="idx3")
+        idx2 = lists.tile([P, SLOTS // 16], U16, name="idx2")
+        idx4 = lists.tile([P, SLOTS // 16], U16, name="idx4")
+        nc.sync.dma_start(idx2[:], offs2)
+        nc.sync.dma_start(idx1[:], offs)
+        nc.sync.dma_start(idx3[:], offs3)
+        nc.sync.dma_start(idx4[:], offs4)
+
+        q_bf = sb.tile([P, Q, PACK], BF16, name="q_bf", align_bytes=64)
+        q_codes = sb.tile([P, Q], U32, name="q_codes", align_bytes=64)
+        q_plane = sb.tile([P, Q], U8, name="q_plane", align_bytes=64)
+        lo, hi = slice(0, Q // 2), slice(Q // 2, Q)
+        nc.vector.tensor_copy(out=q_bf[:, lo, :], in_=q_raw[:, :, lo].rearrange("p j q -> p q j"))
+        nc.scalar.activation(q_bf[:, hi, :], q_raw[:, :, hi].rearrange("p j q -> p q j"), COPY)
+        for cols in (lo, hi):
+            nc.vector.quantize_mx(
+                out=q_codes[:, cols].bitcast(FP8X4),
+                scales=q_plane[:, cols],
+                in_=q_bf[:, cols, :].rearrange("p q j -> p (q j)"),
+            )
+
+        def scores(name, rhs, rhs_scale):
+            bank = psum.tile([P, N], F32, name=name)
+            nc.tensor.matmul_mx(
+                out=bank[:], lhsT=q_codes[:].bitcast(FP8X4), lhsT_scale=q_plane[:],
+                rhs=rhs, rhs_scale=rhs_scale, start=True, stop=True,
+            )
+            return bank
+
+        a = sb.tile([P, T], F32, name="a")
+        b = sb.tile([P, U], F32, name="b")
+        for c in range(T // N):
+            cols = slice(c * N, (c + 1) * N)
+            bank = scores("a%d" % c, key_codes[:, 2 * c * N : 2 * (c + 1) * N].bitcast(FP4X4), key_plane[:, cols])
+            if c % 2 == 0:
+                nc.vector.tensor_copy(out=a[:, cols], in_=bank[:])
+            else:
+                nc.scalar.activation(a[:, cols], bank[:], COPY)
+        for c in range(U // N):
+            cols = slice(c * N, (c + 1) * N)
+            bank = scores("b%d" % c, note_codes[:, cols].bitcast(FP8X4), note_plane[:, cols])
+            nc.scalar.activation(b[:, cols], bank[:], COPY)
+
+        def half(idx, h):
+            return idx[:, h * HCOLS : (h + 1) * HCOLS]
+
+        a1 = sb.tile([P, SLOTS], F32, name="a1")
+        b2 = sb.tile([P, SLOTS], F32, name="b2")
+        for h in range(2):
+            slots = slice(h * HALF, (h + 1) * HALF)
+            a3 = sb.tile([P, HALF], F32, name="a3_%d" % h)
+            if h == 0:
+                nc.vector.tensor_copy(a1[:, slots], a[:].indirect(half(idx1, h)))
+                nc.vector.tensor_copy(a3[:], a[:].indirect(half(idx3, h)))
+                nc.scalar.activation(b2[:, slots], b[:].indirect(half(idx2, h)), COPY)
+            else:
+                nc.scalar.activation(a1[:, slots], a[:].indirect(half(idx1, h)), COPY)
+                nc.scalar.activation(a3[:], a[:].indirect(half(idx3, h)), COPY)
+                nc.scalar.activation(b2[:, slots], b[:].indirect(half(idx2, h)), COPY)
+            low = sb.tile([P, HALF], F32, name="low%d" % h)
+            m1 = sb.tile([P, HALF], F32, name="m1_%d" % h)
+            nc.vector.tensor_tensor(low[:], a1[:, slots], a3[:], ALU.min)
+            nc.vector.tensor_tensor(m1[:], low[:], b2[:, slots], ALU.max)
+            nc.vector.tensor_copy(f1[:].indirect(half(idx3, h)), m1[:])
+
+        aa = sb.tile([P, T], F32, name="aa")
+        nc.vector.tensor_tensor(aa[:], a[:], f1[:], ALU.subtract)
+        w = sb.tile([P, SLOTS], F32, name="w")
+        nc.vector.tensor_tensor(w[:], a1[:], b2[:], ALU.max)
+
+        y0 = sb.tile([P, HALF], F32, name="y0")
+        y1 = sb.tile([P, HALF], F32, name="y1")
+        aa4 = sb.tile([P, HALF], F32, name="aa4")
+        nc.scalar.activation(aa4[:], aa[:].indirect(half(idx4, 1)), COPY)
+        nc.vector.tensor_tensor(y0[:], aa[:].indirect(half(idx4, 0)), w[:, 0:HALF], ALU.add)
+        nc.sync.dma_start(out=out[:, 0:HALF], in_=y0[:])
+        nc.vector.tensor_tensor(y1[:], aa4[:], w[:, HALF:SLOTS], ALU.add)
+        nc.scalar.dma_start(out=out[:, HALF:SLOTS], in_=y1[:])

@@ -44,10 +44,10 @@ def tile_attend_betterworse_two_kernel(
 
         q_raw = sb.tile([P, PACK, Q], F32, name="q_raw")
         nc.sync.dma_start(out=q_raw[:], in_=query.rearrange("(p j) q -> p j q", j=PACK))
-        for r in range(4):
-            load_scale_rows(key_plane, keys_scales, r)
         key_codes = sb.tile([P, 2 * T], U8, name="key_codes", align_bytes=64)
         nc.sync.dma_start(out=key_codes[:].bitcast(I32), in_=keys_words[0].bitcast(I32))
+        for r in range(4):
+            load_scale_rows(key_plane, keys_scales, r)
         note_codes = sb.tile([P, U], U32, name="note_codes", align_bytes=64)
         nc.sync.dma_start(
             out=note_codes[:].bitcast(I32), in_=notes_words[0].rearrange("p u j -> p (u j)").bitcast(I32)
@@ -59,8 +59,8 @@ def tile_attend_betterworse_two_kernel(
         idx2 = lists.tile([P, SLOTS // 16], U16, name="idx2")
         idx4 = lists.tile([P, SLOTS // 16], U16, name="idx4")
         nc.sync.dma_start(idx2[:], offs2)
-        nc.sync.dma_start(idx1[:], offs)
         nc.sync.dma_start(idx3[:], offs3)
+        nc.sync.dma_start(idx1[:], offs)
         nc.sync.dma_start(idx4[:], offs4)
 
         q_bf = sb.tile([P, Q, PACK], BF16, name="q_bf", align_bytes=64)
@@ -89,47 +89,59 @@ def tile_attend_betterworse_two_kernel(
         for c in range(T // N):
             cols = slice(c * N, (c + 1) * N)
             bank = scores("a%d" % c, key_codes[:, 2 * c * N : 2 * (c + 1) * N].bitcast(FP4X4), key_plane[:, cols])
-            if c % 2 == 0:
+            if c % 2 == 1:
                 nc.vector.tensor_copy(out=a[:, cols], in_=bank[:])
             else:
                 nc.scalar.activation(a[:, cols], bank[:], COPY)
         for c in range(U // N):
             cols = slice(c * N, (c + 1) * N)
             bank = scores("b%d" % c, note_codes[:, cols].bitcast(FP8X4), note_plane[:, cols])
-            nc.scalar.activation(b[:, cols], bank[:], COPY)
+            if c == 0:
+                nc.vector.tensor_copy(out=b[:, cols], in_=bank[:])
+            else:
+                nc.scalar.activation(b[:, cols], bank[:], COPY)
 
         def half(idx, h):
             return idx[:, h * HCOLS : (h + 1) * HCOLS]
 
-        a1 = sb.tile([P, SLOTS], F32, name="a1")
-        b2 = sb.tile([P, SLOTS], F32, name="b2")
-        for h in range(2):
-            slots = slice(h * HALF, (h + 1) * HALF)
-            a3 = sb.tile([P, HALF], F32, name="a3_%d" % h)
-            if h == 0:
-                nc.vector.tensor_copy(a1[:, slots], a[:].indirect(half(idx1, h)))
-                nc.vector.tensor_copy(a3[:], a[:].indirect(half(idx3, h)))
-                nc.scalar.activation(b2[:, slots], b[:].indirect(half(idx2, h)), COPY)
-            else:
-                nc.scalar.activation(a1[:, slots], a[:].indirect(half(idx1, h)), COPY)
-                nc.scalar.activation(a3[:], a[:].indirect(half(idx3, h)), COPY)
-                nc.scalar.activation(b2[:, slots], b[:].indirect(half(idx2, h)), COPY)
-            low = sb.tile([P, HALF], F32, name="low%d" % h)
-            m1 = sb.tile([P, HALF], F32, name="m1_%d" % h)
-            nc.vector.tensor_tensor(low[:], a1[:, slots], a3[:], ALU.min)
-            nc.vector.tensor_tensor(m1[:], low[:], b2[:, slots], ALU.max)
-            nc.vector.tensor_copy(f1[:].indirect(half(idx3, h)), m1[:])
+        def piece(idx, lo_slot, hi_slot):
+            return idx[:, lo_slot // 16 : hi_slot // 16]
+
+        w0 = sb.tile([P, HALF], F32, name="w0")
+        w1 = sb.tile([P, HALF], F32, name="w1")
+        a3_0 = sb.tile([P, HALF], F32, name="a3_0")
+        a3_1 = sb.tile([P, HALF], F32, name="a3_1")
+        b2_0 = sb.tile([P, HALF], F32, name="b2_0")
+        low = sb.tile([P, HALF], F32, name="low")
+        m1_0 = sb.tile([P, HALF], F32, name="m1_0")
+        m1_1 = sb.tile([P, HALF], F32, name="m1_1")
+        QUART = HALF // 2
+
+        nc.vector.tensor_copy(a3_0[:], a[:].indirect(half(idx3, 0)))
+        nc.vector.tensor_copy(w0[:], a[:].indirect(half(idx1, 0)))
+        nc.scalar.activation(b2_0[:], b[:].indirect(half(idx2, 0)), COPY)
+        nc.scalar.activation(a3_1[:], a[:].indirect(half(idx3, 1)), COPY)
+        nc.scalar.activation(w1[:], a[:].indirect(half(idx1, 1)), COPY)
+        nc.vector.tensor_tensor(low[:], w0[:], a3_0[:], ALU.min)
+        b2_1 = a3_0
+        nc.scalar.activation(b2_1[:], b[:].indirect(half(idx2, 1)), COPY)
+        nc.vector.tensor_tensor(m1_0[:], low[:], b2_0[:], ALU.max)
+        nc.vector.tensor_tensor(w0[:], w0[:], b2_0[:], ALU.max)
+        nc.vector.tensor_copy(f1[:].indirect(piece(idx3, 0, QUART)), m1_0[:, 0:QUART])
+        nc.vector.tensor_tensor(low[:], w1[:], a3_1[:], ALU.min)
+        nc.vector.tensor_copy(f1[:].indirect(piece(idx3, QUART, HALF)), m1_0[:, QUART:HALF])
+        nc.vector.tensor_tensor(m1_1[:], low[:], b2_1[:], ALU.max)
+        nc.vector.tensor_tensor(w1[:], w1[:], b2_1[:], ALU.max)
+        nc.vector.tensor_copy(f1[:].indirect(half(idx3, 1)), m1_1[:])
 
         aa = sb.tile([P, T], F32, name="aa")
         nc.vector.tensor_tensor(aa[:], a[:], f1[:], ALU.subtract)
-        w = sb.tile([P, SLOTS], F32, name="w")
-        nc.vector.tensor_tensor(w[:], a1[:], b2[:], ALU.max)
 
         y0 = sb.tile([P, HALF], F32, name="y0")
         y1 = sb.tile([P, HALF], F32, name="y1")
         aa4 = sb.tile([P, HALF], F32, name="aa4")
         nc.scalar.activation(aa4[:], aa[:].indirect(half(idx4, 1)), COPY)
-        nc.vector.tensor_tensor(y0[:], aa[:].indirect(half(idx4, 0)), w[:, 0:HALF], ALU.add)
+        nc.vector.tensor_tensor(y0[:], aa[:].indirect(half(idx4, 0)), w0[:], ALU.add)
         nc.sync.dma_start(out=out[:, 0:HALF], in_=y0[:])
-        nc.vector.tensor_tensor(y1[:], aa4[:], w[:, HALF:SLOTS], ALU.add)
+        nc.vector.tensor_tensor(y1[:], aa4[:], w1[:], ALU.add)
         nc.scalar.dma_start(out=out[:, HALF:SLOTS], in_=y1[:])

@@ -45,8 +45,10 @@ def tile_attend_betterworse_two_kernel(
         q_raw = sb.tile([P, PACK, Q], F32, name="q_raw")
         nc.sync.dma_start(out=q_raw[:], in_=query.rearrange("(p j) q -> p j q", j=PACK))
         key_codes = sb.tile([P, 2 * T], U8, name="key_codes", align_bytes=64)
+        for r in range(2):
+            load_scale_rows(key_plane, keys_scales, r)
         nc.sync.dma_start(out=key_codes[:].bitcast(I32), in_=keys_words[0].bitcast(I32))
-        for r in range(4):
+        for r in range(2, 4):
             load_scale_rows(key_plane, keys_scales, r)
         note_codes = sb.tile([P, U], U32, name="note_codes", align_bytes=64)
         nc.sync.dma_start(
@@ -86,9 +88,11 @@ def tile_attend_betterworse_two_kernel(
 
         a = sb.tile([P, T], F32, name="a")
         b = sb.tile([P, U], F32, name="b")
+        a_banks = []
         for c in range(T // N):
             cols = slice(c * N, (c + 1) * N)
             bank = scores("a%d" % c, key_codes[:, 2 * c * N : 2 * (c + 1) * N].bitcast(FP4X4), key_plane[:, cols])
+            a_banks.append(bank)
             if c % 2 == 1:
                 nc.vector.tensor_copy(out=a[:, cols], in_=bank[:])
             else:
@@ -135,7 +139,11 @@ def tile_attend_betterworse_two_kernel(
         nc.vector.tensor_copy(f1[:].indirect(half(idx3, 1)), m1_1[:])
 
         aa = sb.tile([P, T], F32, name="aa")
-        nc.vector.tensor_tensor(aa[:], a[:], f1[:], ALU.subtract)
+        SPLIT = 768
+        nc.gpsimd.tensor_tensor(aa[:, SPLIT:T], a[:, SPLIT:T], f1[:, SPLIT:T], ALU.subtract)
+        for c0 in range(0, SPLIT, N):
+            c1 = min(c0 + N, SPLIT)
+            nc.vector.tensor_tensor(aa[:, c0:c1], a_banks[c0 // N][:, 0 : c1 - c0], f1[:, c0:c1], ALU.subtract)
 
         y0 = sb.tile([P, HALF], F32, name="y0")
         y1 = sb.tile([P, HALF], F32, name="y1")

@@ -113,29 +113,27 @@ def tile_attend_betterworse_two_kernel(
 
         w0 = sb.tile([P, HALF], F32, name="w0")
         w1 = sb.tile([P, HALF], F32, name="w1")
-        a3_0 = sb.tile([P, HALF], F32, name="a3_0")
-        a3_1 = sb.tile([P, HALF], F32, name="a3_1")
-        b2_0 = sb.tile([P, HALF], F32, name="b2_0")
+        a3 = sb.tile([P, HALF], F32, name="a3")
+        b2 = sb.tile([P, HALF], F32, name="b2")
         low = sb.tile([P, HALF], F32, name="low")
         m1_0 = sb.tile([P, HALF], F32, name="m1_0")
         m1_1 = sb.tile([P, HALF], F32, name="m1_1")
         QUART = HALF // 2
 
-        nc.vector.tensor_copy(a3_0[:], a[:].indirect(half(idx3, 0)))
+        nc.vector.tensor_copy(a3[:], a[:].indirect(half(idx3, 0)))
         nc.vector.tensor_copy(w0[:], a[:].indirect(half(idx1, 0)))
-        nc.scalar.activation(b2_0[:], b[:].indirect(half(idx2, 0)), COPY)
-        nc.scalar.activation(a3_1[:], a[:].indirect(half(idx3, 1)), COPY)
+        nc.scalar.activation(b2[:], b[:].indirect(half(idx2, 0)), COPY)
         nc.scalar.activation(w1[:], a[:].indirect(half(idx1, 1)), COPY)
-        nc.vector.tensor_tensor(low[:], w0[:], a3_0[:], ALU.min)
-        b2_1 = a3_0
-        nc.scalar.activation(b2_1[:], b[:].indirect(half(idx2, 1)), COPY)
-        nc.vector.tensor_tensor(m1_0[:], low[:], b2_0[:], ALU.max)
-        nc.vector.tensor_tensor(w0[:], w0[:], b2_0[:], ALU.max)
+        nc.vector.tensor_tensor(low[:], w0[:], a3[:], ALU.min)
+        nc.scalar.activation(a3[:], a[:].indirect(half(idx3, 1)), COPY)
+        nc.vector.tensor_tensor(m1_0[:], low[:], b2[:], ALU.max)
+        nc.vector.tensor_tensor(w0[:], w0[:], b2[:], ALU.max)
+        nc.scalar.activation(b2[:], b[:].indirect(half(idx2, 1)), COPY)
         nc.vector.tensor_copy(f1[:].indirect(piece(idx3, 0, QUART)), m1_0[:, 0:QUART])
-        nc.vector.tensor_tensor(low[:], w1[:], a3_1[:], ALU.min)
+        nc.vector.tensor_tensor(low[:], w1[:], a3[:], ALU.min)
         nc.vector.tensor_copy(f1[:].indirect(piece(idx3, QUART, HALF)), m1_0[:, QUART:HALF])
-        nc.vector.tensor_tensor(m1_1[:], low[:], b2_1[:], ALU.max)
-        nc.vector.tensor_tensor(w1[:], w1[:], b2_1[:], ALU.max)
+        nc.vector.tensor_tensor(m1_1[:], low[:], b2[:], ALU.max)
+        nc.vector.tensor_tensor(w1[:], w1[:], b2[:], ALU.max)
         nc.vector.tensor_copy(f1[:].indirect(half(idx3, 1)), m1_1[:])
 
         aa = sb.tile([P, T], F32, name="aa")

@@ -18,9 +18,12 @@ COPY = mybir.ActivationFunctionType.Copy
 
 P = 128
 PACK = 4
+QUADRANT = 32
+SCALE_ROWS = 4
+GROUP = 16
 N = 256
 HALF = SLOTS // 2
-HCOLS = HALF // 16
+QUARTER = SLOTS // 4
 
 
 def tile_attend_betterworse_two_kernel(
@@ -40,42 +43,45 @@ def tile_attend_betterworse_two_kernel(
         nc.vector.memset(f1[:], 0.0)
 
         def load_scale_rows(plane, scales, r):
-            nc.sync.dma_start(out=plane[r:P:32, :].bitcast(I32), in_=scales[0, r:16:4, :].bitcast(I32))
+            nc.sync.dma_start(
+                out=plane[r:P:QUADRANT, :].bitcast(I32),
+                in_=scales[0, r : D // 32 : SCALE_ROWS, :].bitcast(I32),
+            )
 
         q_raw = sb.tile([P, PACK, Q], F32, name="q_raw")
         nc.sync.dma_start(out=q_raw[:], in_=query.rearrange("(p j) q -> p j q", j=PACK))
         key_codes = sb.tile([P, 2 * T], U8, name="key_codes", align_bytes=64)
-        for r in range(2):
+        for r in range(SCALE_ROWS // 2):
             load_scale_rows(key_plane, keys_scales, r)
         nc.sync.dma_start(out=key_codes[:].bitcast(I32), in_=keys_words[0].bitcast(I32))
-        for r in range(2, 4):
+        for r in range(SCALE_ROWS // 2, SCALE_ROWS):
             load_scale_rows(key_plane, keys_scales, r)
-        note_codes = sb.tile([P, U], U32, name="note_codes", align_bytes=64)
+        note_codes = sb.tile([P, U], U32, name="note_codes", tag="notes_then_a3", align_bytes=64)
         nc.sync.dma_start(
             out=note_codes[:].bitcast(I32), in_=notes_words[0].rearrange("p u j -> p (u j)").bitcast(I32)
         )
-        for r in range(4):
+        for r in range(SCALE_ROWS):
             load_scale_rows(note_plane, notes_scales, r)
-        idx1 = lists.tile([P, SLOTS // 16], U16, name="idx1")
-        idx3 = lists.tile([P, SLOTS // 16], U16, name="idx3")
-        idx2 = lists.tile([P, SLOTS // 16], U16, name="idx2")
-        idx4 = lists.tile([P, SLOTS // 16], U16, name="idx4")
-        nc.sync.dma_start(idx2[:], offs2)
+        idx1 = lists.tile([P, SLOTS // GROUP], U16, name="idx1")
+        idx3 = lists.tile([P, SLOTS // GROUP], U16, name="idx3")
+        idx2 = lists.tile([P, SLOTS // GROUP], U16, name="idx2")
+        idx4 = lists.tile([P, SLOTS // GROUP], U16, name="idx4")
         nc.sync.dma_start(idx3[:], offs3)
         nc.sync.dma_start(idx1[:], offs)
+        nc.sync.dma_start(idx2[:], offs2)
         nc.sync.dma_start(idx4[:], offs4)
 
         q_bf = sb.tile([P, Q, PACK], BF16, name="q_bf", align_bytes=64)
         q_codes = sb.tile([P, Q], U32, name="q_codes", align_bytes=64)
         q_plane = sb.tile([P, Q], U8, name="q_plane", align_bytes=64)
-        lo, hi = slice(0, Q // 2), slice(Q // 2, Q)
-        nc.vector.tensor_copy(out=q_bf[:, lo, :], in_=q_raw[:, :, lo].rearrange("p j q -> p q j"))
-        nc.scalar.activation(q_bf[:, hi, :], q_raw[:, :, hi].rearrange("p j q -> p q j"), COPY)
-        for cols in (lo, hi):
+        rows_lo, rows_hi = slice(0, Q // 2), slice(Q // 2, Q)
+        nc.vector.tensor_copy(out=q_bf[:, rows_lo, :], in_=q_raw[:, :, rows_lo].rearrange("p j q -> p q j"))
+        nc.scalar.activation(q_bf[:, rows_hi, :], q_raw[:, :, rows_hi].rearrange("p j q -> p q j"), COPY)
+        for rows in (rows_lo, rows_hi):
             nc.vector.quantize_mx(
-                out=q_codes[:, cols].bitcast(FP8X4),
-                scales=q_plane[:, cols],
-                in_=q_bf[:, cols, :].rearrange("p q j -> p (q j)"),
+                out=q_codes[:, rows].bitcast(FP8X4),
+                scales=q_plane[:, rows],
+                in_=q_bf[:, rows, :].rearrange("p q j -> p (q j)"),
             )
 
         def scores(name, rhs, rhs_scale):
@@ -85,6 +91,9 @@ def tile_attend_betterworse_two_kernel(
                 rhs=rhs, rhs_scale=rhs_scale, start=True, stop=True,
             )
             return bank
+
+        def entries(idx, first, count):
+            return idx[:, first // GROUP : (first + count) // GROUP]
 
         a = sb.tile([P, T], F32, name="a")
         b = sb.tile([P, U], F32, name="b")
@@ -97,57 +106,59 @@ def tile_attend_betterworse_two_kernel(
                 nc.vector.tensor_copy(out=a[:, cols], in_=bank[:])
             else:
                 nc.scalar.activation(a[:, cols], bank[:], COPY)
+
+        a3_0 = sb.tile([P, HALF], F32, name="a3_0", tag="a3_then_second_half")
         for c in range(U // N):
             cols = slice(c * N, (c + 1) * N)
             bank = scores("b%d" % c, note_codes[:, cols].bitcast(FP8X4), note_plane[:, cols])
-            if c == 0:
+            if c in (0, U // N - 1):
                 nc.vector.tensor_copy(out=b[:, cols], in_=bank[:])
             else:
                 nc.scalar.activation(b[:, cols], bank[:], COPY)
+            if c == 0:
+                nc.vector.tensor_copy(a3_0[:], a[:].indirect(entries(idx3, 0, HALF)))
 
-        def half(idx, h):
-            return idx[:, h * HCOLS : (h + 1) * HCOLS]
-
-        def piece(idx, lo_slot, hi_slot):
-            return idx[:, lo_slot // 16 : hi_slot // 16]
-
-        w0 = sb.tile([P, HALF], F32, name="w0")
-        w1 = sb.tile([P, HALF], F32, name="w1")
-        a3 = sb.tile([P, HALF], F32, name="a3")
-        b2 = sb.tile([P, HALF], F32, name="b2")
+        a1_0 = sb.tile([P, HALF], F32, name="a1_0")
+        a3_1 = sb.tile([P, HALF], F32, name="a3_1", tag="notes_then_a3", align_bytes=64)
+        b2_0 = sb.tile([P, HALF], F32, name="b2_0")
         low = sb.tile([P, HALF], F32, name="low")
         m1_0 = sb.tile([P, HALF], F32, name="m1_0")
         m1_1 = sb.tile([P, HALF], F32, name="m1_1")
-        QUART = HALF // 2
 
-        nc.vector.tensor_copy(a3[:], a[:].indirect(half(idx3, 0)))
-        nc.vector.tensor_copy(w0[:], a[:].indirect(half(idx1, 0)))
-        nc.scalar.activation(b2[:], b[:].indirect(half(idx2, 0)), COPY)
-        nc.scalar.activation(w1[:], a[:].indirect(half(idx1, 1)), COPY)
-        nc.vector.tensor_tensor(low[:], w0[:], a3[:], ALU.min)
-        nc.scalar.activation(a3[:], a[:].indirect(half(idx3, 1)), COPY)
-        nc.vector.tensor_tensor(m1_0[:], low[:], b2[:], ALU.max)
-        nc.vector.tensor_tensor(w0[:], w0[:], b2[:], ALU.max)
-        nc.scalar.activation(b2[:], b[:].indirect(half(idx2, 1)), COPY)
-        nc.vector.tensor_copy(f1[:].indirect(piece(idx3, 0, QUART)), m1_0[:, 0:QUART])
-        nc.vector.tensor_tensor(low[:], w1[:], a3[:], ALU.min)
-        nc.vector.tensor_copy(f1[:].indirect(piece(idx3, QUART, HALF)), m1_0[:, QUART:HALF])
-        nc.vector.tensor_tensor(m1_1[:], low[:], b2[:], ALU.max)
-        nc.vector.tensor_tensor(w1[:], w1[:], b2[:], ALU.max)
-        nc.vector.tensor_copy(f1[:].indirect(half(idx3, 1)), m1_1[:])
+        nc.vector.tensor_copy(a3_1[:], a[:].indirect(entries(idx3, HALF, HALF)))
+        nc.scalar.activation(a1_0[:], a[:].indirect(entries(idx1, 0, HALF)), COPY)
+        nc.scalar.activation(b2_0[:], b[:].indirect(entries(idx2, 0, HALF)), COPY)
+        nc.vector.tensor_tensor(low[:], a1_0[:], a3_0[:], ALU.min)
+        second = sb.tile([P, 2, HALF], F32, name="second", tag="a3_then_second_half")
+        a1_1, b2_1 = second[:, 0, :], second[:, 1, :]
+        nc.scalar.activation(a1_1, a[:].indirect(entries(idx1, HALF, HALF)), COPY)
+        nc.scalar.activation(b2_1, b[:].indirect(entries(idx2, HALF, HALF)), COPY)
+
+        for first in (0, QUARTER):
+            part = slice(first, first + QUARTER)
+            nc.vector.tensor_tensor(m1_0[:, part], low[:, part], b2_0[:, part], ALU.max)
+        nc.vector.tensor_copy(f1[:].indirect(entries(idx3, 0, QUARTER)), m1_0[:, 0:QUARTER])
+        nc.vector.tensor_tensor(low[:], a1_1, a3_1[:], ALU.min)
+        nc.vector.tensor_copy(f1[:].indirect(entries(idx3, QUARTER, QUARTER)), m1_0[:, QUARTER:HALF])
+        nc.vector.tensor_tensor(m1_1[:], low[:], b2_1, ALU.max)
+        w_1 = a1_1
+        nc.vector.tensor_tensor(w_1, a1_1, b2_1, ALU.max)
+        nc.vector.tensor_copy(f1[:].indirect(entries(idx3, HALF, HALF)), m1_1[:])
+        w_0 = low
+        nc.vector.tensor_tensor(w_0[:], a1_0[:], b2_0[:], ALU.max)
 
         aa = sb.tile([P, T], F32, name="aa")
-        SPLIT = 768
-        nc.gpsimd.tensor_tensor(aa[:, SPLIT:T], a[:, SPLIT:T], f1[:, SPLIT:T], ALU.subtract)
-        for c0 in range(0, SPLIT, N):
-            c1 = min(c0 + N, SPLIT)
-            nc.vector.tensor_tensor(aa[:, c0:c1], a_banks[c0 // N][:, 0 : c1 - c0], f1[:, c0:c1], ALU.subtract)
+        last = slice(T - N, T)
+        nc.gpsimd.tensor_tensor(aa[:, last], a[:, last], f1[:, last], ALU.subtract)
+        for c in range(T // N - 1):
+            cols = slice(c * N, (c + 1) * N)
+            nc.vector.tensor_tensor(aa[:, cols], a_banks[c][:], f1[:, cols], ALU.subtract)
 
-        y0 = sb.tile([P, HALF], F32, name="y0")
-        y1 = sb.tile([P, HALF], F32, name="y1")
-        aa4 = sb.tile([P, HALF], F32, name="aa4")
-        nc.scalar.activation(aa4[:], aa[:].indirect(half(idx4, 1)), COPY)
-        nc.vector.tensor_tensor(y0[:], aa[:].indirect(half(idx4, 0)), w0[:], ALU.add)
-        nc.sync.dma_start(out=out[:, 0:HALF], in_=y0[:])
-        nc.vector.tensor_tensor(y1[:], aa4[:], w1[:], ALU.add)
-        nc.scalar.dma_start(out=out[:, HALF:SLOTS], in_=y1[:])
+        out_0 = sb.tile([P, HALF], F32, name="out_0")
+        out_1 = sb.tile([P, HALF], F32, name="out_1")
+        aa4_1 = sb.tile([P, HALF], F32, name="aa4_1")
+        nc.scalar.activation(aa4_1[:], aa[:].indirect(entries(idx4, HALF, HALF)), COPY)
+        nc.vector.tensor_tensor(out_0[:], aa[:].indirect(entries(idx4, 0, HALF)), w_0[:], ALU.add)
+        nc.sync.dma_start(out=out[:, 0:HALF], in_=out_0[:])
+        nc.vector.tensor_tensor(out_1[:], aa4_1[:], w_1, ALU.add)
+        nc.sync.dma_start(out=out[:, HALF:SLOTS], in_=out_1[:])

from contextlib import ExitStack

import concourse.mybir as mybir

D, T, U, SLOTS, Q = 512, 1024, 1024, 512, 128
FLOPS = 2 * Q * D * (T + U)

F32 = mybir.dt.float32
BF16 = mybir.dt.bfloat16
I32 = mybir.dt.int32
U32 = mybir.dt.uint32
U16 = mybir.dt.uint16
U8 = mybir.dt.uint8
FP8X4 = mybir.dt.float8_e4m3fn_x4
FP4X4 = mybir.dt.float4_e2m1fn_x4
ALU = mybir.AluOpType
COPY = mybir.ActivationFunctionType.Copy

P = 128
PACK = 4
QUADRANT = 32
SCALE_ROWS = 4
GROUP = 16
N = 256
HALF = SLOTS // 2
QUARTER = SLOTS // 4


def tile_attend_betterworse_two_kernel(
    tc, query, keys_words, keys_scales, notes_words, notes_scales, offs, offs2, offs3, offs4, out
):
    nc = tc.nc
    with ExitStack() as ctx:
        lists = ctx.enter_context(tc.tile_pool(name="lists", bufs=1))
        sb = ctx.enter_context(tc.tile_pool(name="sb", bufs=1))
        psum = ctx.enter_context(tc.psum_pool(name="psum", bufs=1))

        key_plane = sb.tile([P, T], U8, name="key_plane", align_bytes=64)
        note_plane = sb.tile([P, U], U8, name="note_plane", align_bytes=64)
        f1 = sb.tile([P, T], F32, name="f1")
        nc.vector.memset(key_plane[:].bitcast(U32), 0)
        nc.vector.memset(note_plane[:].bitcast(U32), 0)
        nc.vector.memset(f1[:], 0.0)

        def load_scale_rows(plane, scales, r):
            nc.sync.dma_start(
                out=plane[r:P:QUADRANT, :].bitcast(I32),
                in_=scales[0, r : D // 32 : SCALE_ROWS, :].bitcast(I32),
            )

        q_raw = sb.tile([P, PACK, Q], F32, name="q_raw")
        nc.sync.dma_start(out=q_raw[:], in_=query.rearrange("(p j) q -> p j q", j=PACK))
        key_codes = sb.tile([P, 2 * T], U8, name="key_codes", align_bytes=64)
        for r in range(SCALE_ROWS // 2):
            load_scale_rows(key_plane, keys_scales, r)
        nc.sync.dma_start(out=key_codes[:].bitcast(I32), in_=keys_words[0].bitcast(I32))
        for r in range(SCALE_ROWS // 2, SCALE_ROWS):
            load_scale_rows(key_plane, keys_scales, r)
        note_codes = sb.tile([P, U], U32, name="note_codes", tag="notes_then_a3", align_bytes=64)
        nc.sync.dma_start(
            out=note_codes[:].bitcast(I32), in_=notes_words[0].rearrange("p u j -> p (u j)").bitcast(I32)
        )
        for r in range(SCALE_ROWS):
            load_scale_rows(note_plane, notes_scales, r)
        idx1 = lists.tile([P, SLOTS // GROUP], U16, name="idx1")
        idx3 = lists.tile([P, SLOTS // GROUP], U16, name="idx3")
        idx2 = lists.tile([P, SLOTS // GROUP], U16, name="idx2")
        idx4 = lists.tile([P, SLOTS // GROUP], U16, name="idx4")
        nc.sync.dma_start(idx3[:], offs3)
        nc.sync.dma_start(idx1[:], offs)
        nc.sync.dma_start(idx2[:], offs2)
        nc.sync.dma_start(idx4[:], offs4)

        q_bf = sb.tile([P, Q, PACK], BF16, name="q_bf", align_bytes=64)
        q_codes = sb.tile([P, Q], U32, name="q_codes", align_bytes=64)
        q_plane = sb.tile([P, Q], U8, name="q_plane", align_bytes=64)
        rows_lo, rows_hi = slice(0, Q // 2), slice(Q // 2, Q)
        nc.vector.tensor_copy(out=q_bf[:, rows_lo, :], in_=q_raw[:, :, rows_lo].rearrange("p j q -> p q j"))
        nc.scalar.activation(q_bf[:, rows_hi, :], q_raw[:, :, rows_hi].rearrange("p j q -> p q j"), COPY)
        for rows in (rows_lo, rows_hi):
            nc.vector.quantize_mx(
                out=q_codes[:, rows].bitcast(FP8X4),
                scales=q_plane[:, rows],
                in_=q_bf[:, rows, :].rearrange("p q j -> p (q j)"),
            )

        def scores(name, rhs, rhs_scale):
            bank = psum.tile([P, N], F32, name=name)
            nc.tensor.matmul_mx(
                out=bank[:], lhsT=q_codes[:].bitcast(FP8X4), lhsT_scale=q_plane[:],
                rhs=rhs, rhs_scale=rhs_scale, start=True, stop=True,
            )
            return bank

        def entries(idx, first, count):
            return idx[:, first // GROUP : (first + count) // GROUP]

        a = sb.tile([P, T], F32, name="a")
        b = sb.tile([P, U], F32, name="b")
        a_banks = []
        for c in range(T // N):
            cols = slice(c * N, (c + 1) * N)
            bank = scores("a%d" % c, key_codes[:, 2 * c * N : 2 * (c + 1) * N].bitcast(FP4X4), key_plane[:, cols])
            a_banks.append(bank)
            if c % 2 == 1:
                nc.vector.tensor_copy(out=a[:, cols], in_=bank[:])
            else:
                nc.scalar.activation(a[:, cols], bank[:], COPY)

        a3_0 = sb.tile([P, HALF], F32, name="a3_0", tag="a3_then_second_half")
        for c in range(U // N):
            cols = slice(c * N, (c + 1) * N)
            bank = scores("b%d" % c, note_codes[:, cols].bitcast(FP8X4), note_plane[:, cols])
            if c in (0, U // N - 1):
                nc.vector.tensor_copy(out=b[:, cols], in_=bank[:])
            else:
                nc.scalar.activation(b[:, cols], bank[:], COPY)
            if c == 0:
                nc.vector.tensor_copy(a3_0[:], a[:].indirect(entries(idx3, 0, HALF)))

        a1_0 = sb.tile([P, HALF], F32, name="a1_0")
        a3_1 = sb.tile([P, HALF], F32, name="a3_1", tag="notes_then_a3", align_bytes=64)
        b2_0 = sb.tile([P, HALF], F32, name="b2_0")
        low = sb.tile([P, HALF], F32, name="low")
        m1_0 = sb.tile([P, HALF], F32, name="m1_0")
        m1_1 = sb.tile([P, HALF], F32, name="m1_1")

        nc.vector.tensor_copy(a3_1[:], a[:].indirect(entries(idx3, HALF, HALF)))
        nc.scalar.activation(a1_0[:], a[:].indirect(entries(idx1, 0, HALF)), COPY)
        nc.scalar.activation(b2_0[:], b[:].indirect(entries(idx2, 0, HALF)), COPY)
        nc.vector.tensor_tensor(low[:], a1_0[:], a3_0[:], ALU.min)
        second = sb.tile([P, 2, HALF], F32, name="second", tag="a3_then_second_half")
        a1_1, b2_1 = second[:, 0, :], second[:, 1, :]
        nc.scalar.activation(a1_1, a[:].indirect(entries(idx1, HALF, HALF)), COPY)
        nc.scalar.activation(b2_1, b[:].indirect(entries(idx2, HALF, HALF)), COPY)

        for first in (0, QUARTER):
            part = slice(first, first + QUARTER)
            nc.vector.tensor_tensor(m1_0[:, part], low[:, part], b2_0[:, part], ALU.max)
        nc.vector.tensor_copy(f1[:].indirect(entries(idx3, 0, QUARTER)), m1_0[:, 0:QUARTER])
        nc.vector.tensor_tensor(low[:], a1_1, a3_1[:], ALU.min)
        nc.vector.tensor_copy(f1[:].indirect(entries(idx3, QUARTER, QUARTER)), m1_0[:, QUARTER:HALF])
        nc.vector.tensor_tensor(m1_1[:], low[:], b2_1, ALU.max)
        w_1 = a1_1
        nc.vector.tensor_tensor(w_1, a1_1, b2_1, ALU.max)
        nc.vector.tensor_copy(f1[:].indirect(entries(idx3, HALF, HALF)), m1_1[:])
        w_0 = low
        nc.vector.tensor_tensor(w_0[:], a1_0[:], b2_0[:], ALU.max)

        aa = sb.tile([P, T], F32, name="aa")
        last = slice(T - N, T)
        nc.gpsimd.tensor_tensor(aa[:, last], a[:, last], f1[:, last], ALU.subtract)
        for c in range(T // N - 1):
            cols = slice(c * N, (c + 1) * N)
            nc.vector.tensor_tensor(aa[:, cols], a_banks[c][:], f1[:, cols], ALU.subtract)

        out_0 = sb.tile([P, HALF], F32, name="out_0")
        out_1 = sb.tile([P, HALF], F32, name="out_1")
        aa4_1 = sb.tile([P, HALF], F32, name="aa4_1")
        nc.scalar.activation(aa4_1[:], aa[:].indirect(entries(idx4, HALF, HALF)), COPY)
        nc.vector.tensor_tensor(out_0[:], aa[:].indirect(entries(idx4, 0, HALF)), w_0[:], ALU.add)
        nc.sync.dma_start(out=out[:, 0:HALF], in_=out_0[:])
        nc.vector.tensor_tensor(out_1[:], aa4_1[:], w_1, ALU.add)
        nc.sync.dma_start(out=out[:, HALF:SLOTS], in_=out_1[:])
